import numpy as np
import ml_dtypes


def mxq(x, axis, fmt="e4m3"):
    dtype, down = {"e4m3": (ml_dtypes.float8_e4m3fn, 7), "e5m2": (ml_dtypes.float8_e5m2, 14)}[fmt]
    v = np.moveaxis(np.asarray(x, np.float32).astype(ml_dtypes.bfloat16).astype(np.float64), axis, -1)
    blocks = v.reshape(v.shape[:-1] + (-1, 32))
    amax = np.abs(blocks).max(-1, keepdims=True)
    byte = np.maximum(np.where(amax > 0, np.frexp(amax)[1] - 1 + 127, 0) - down, 1)
    scale = np.exp2(byte - 127.0)
    codes = (blocks / scale).astype(np.float32).astype(dtype).astype(np.float64)
    return np.moveaxis((codes * scale).reshape(v.shape), -1, axis)


WIDE = False


def mx_kscale(k):
    if not WIDE:
        return np.ones(k)
    levels = np.array([10, -10, 5, -5, 0])
    if k % 512:
        return np.exp2(np.random.permutation(np.resize(levels, k // 32))).repeat(32)
    a = np.empty((k // 512, 16))
    for p in range(k // 512):
        a[p, :8] = np.random.permutation(np.resize(levels, 8))
        for g in range(8):
            far = levels[np.abs(levels - a[p, g]) >= 10]
            a[p, g + 8] = far[np.random.randint(len(far))]
    return np.exp2(a.ravel()).repeat(32)


def f64(x):
    return np.asarray(x).astype(np.float64)


def striped(idx):
    return np.tile(np.asarray(idx).reshape(-1, 16).T, (8, 1)).astype(np.uint16)


def unstriped(offs):
    return offs[:16].T.reshape(-1).astype(np.int64)


E2M1 = np.array([0.0, 0.5, 1.0, 1.5, 2.0, 3.0, 4.0, 6.0, -0.0, -0.5, -1.0, -1.5, -2.0, -3.0, -4.0, -6.0])


def pack_weight(w, fmt):
    k, n = w.shape
    w = f64(np.asarray(w, np.float32).astype(ml_dtypes.bfloat16)).reshape(k // 32, 32, n)
    amax = np.abs(w).max(1)
    if fmt == "e4m3":
        byte = np.frexp(amax)[1] - 1 + 127 - 7
    else:
        mant, ex = np.frexp(amax / 6.0)
        byte = np.where(mant > 0.5, ex, ex - 1) + 127
    byte = np.clip(np.where(amax > 0, byte, 1), 1, 254)
    scaled = (w * np.exp2(127.0 - byte)[:, None, :]).reshape(k, n).astype(np.float32)
    by_word = np.ascontiguousarray(scaled.reshape(k // 512, 128, 4, n).transpose(0, 1, 3, 2))
    if fmt == "e4m3":
        words = by_word.astype(ml_dtypes.float8_e4m3fn).view(np.uint8)
    else:
        c = by_word.astype(ml_dtypes.float4_e2m1fn).view(np.uint8) & 0xF
        words = (c[..., 0::2] | (c[..., 1::2] << 4)).reshape(k // 512, 128, 2 * n)
    return np.ascontiguousarray(words), np.ascontiguousarray(byte.astype(np.uint8).reshape(k // 512, 16, n))


def unpack_weight(words, scales, fmt):
    g, _, n = scales.shape
    words = np.ascontiguousarray(words).reshape(g, 128, n, -1)
    if fmt == "e4m3":
        vals = words.view(ml_dtypes.float8_e4m3fn).astype(np.float64)
    else:
        nib = np.empty((g, 128, n, 4), np.uint8)
        nib[..., 0::2] = words & 0xF
        nib[..., 1::2] = words >> 4
        vals = E2M1[nib]
    vals = vals * np.repeat(np.exp2(scales.astype(np.float64) - 127.0), 8, axis=1)[..., None]
    return vals.transpose(0, 1, 3, 2).reshape(g * 512, n)


D, K, T, I, U, Q = 512, 512, 2048, 512, 256, 256


def setup_inputs():
    n = np.random.standard_normal
    idx = np.random.permutation(T)[:I]
    idx2 = np.random.randint(0, U, I)
    fd = mx_kscale(D)
    pkptp = pack_weight(n((D, T)) / fd[:, None], "e4m3")
    return {
        "pts": (n((D, T)) / fd[:, None]).astype(np.float32),
        "mean": (n((D, U)) * 0.7 / fd[:, None]).astype(np.float32),
        "white": (n((D, K)) * 1 / np.sqrt(D) * fd[:, None]).astype(np.float32),
        "pkpt_words": pkptp[0],
        "pkpt_scales": pkptp[1],
        "query": (n((D, Q)) * 1 / np.sqrt(D) * fd[:, None]).astype(np.float32),
        "sharp": (np.random.uniform(0.5, 2.0, (I, 1))).astype(np.float32),
        "offs": striped(idx),
        "offs2": striped(idx2),
    }


def reference(pts, mean, white, pkpt_words, pkpt_scales, query, sharp, offs, offs2):
    idx = unstriped(offs)
    idx2 = unstriped(offs2)
    pkptu = unpack_weight(pkpt_words, pkpt_scales, "e4m3")
    xc = f64(pts)[:, idx] - f64(mean)[:, idx2]
    xcq = mxq(xc, 0, "e4m3")
    whiteq = mxq(f64(white), 0, "e4m3")
    z = xcq.T @ whiteq
    en = np.mean(np.square(z), axis=1, keepdims=True) * f64(sharp)
    pkptidxg = pkptu[:, idx]
    queryq = mxq(f64(query), 0, "e4m3")
    a = pkptidxg.T @ queryq
    y = a - en
    return y

@@ -1,0 +1,144 @@
+from contextlib import ExitStack
+
+import concourse.mybir as mybir
+from concourse.masks import make_identity
+
+D, K, T, I, U, Q = 512, 512, 2048, 512, 256, 256
+FLOPS = 2 * I * D * (K + Q)
+
+F32 = mybir.dt.float32
+BF16 = mybir.dt.bfloat16
+I32 = mybir.dt.int32
+U32 = mybir.dt.uint32
+U16 = mybir.dt.uint16
+U8 = mybir.dt.uint8
+FP8X4 = mybir.dt.float8_e4m3fn_x4
+ALU = mybir.AluOpType
+ACT = mybir.ActivationFunctionType
+
+P = 128
+PACK = 4
+TILES = I // P
+COLS = P // 16
+MEAN_WINDOW = 704
+
+
+def tile_attend_energyscores_kernel(tc, pts, mean, white, pkpt_words, pkpt_scales, query, sharp, offs, offs2, out):
+    nc = tc.nc
+    with ExitStack() as ctx:
+        sb = ctx.enter_context(tc.tile_pool(name="sb", bufs=1))
+        psum = ctx.enter_context(tc.psum_pool(name="psum", bufs=4))
+
+        idx = sb.tile([P, I // 16], U16, name="idx")
+        idx2 = sb.tile([P, I // 16], U16, name="idx2")
+        mean_sb = sb.tile([P, (PACK - 1) * U + MEAN_WINDOW], F32, name="mean_sb")
+        white_sb = sb.tile([P, PACK, K], F32, name="white_sb")
+        query_sb = sb.tile([P, PACK, Q], F32, name="query_sb")
+        planes = [sb.tile([P, T], F32, name=f"pts{t}") for t in range(PACK)]
+        words = sb.tile([P, T], U32, name="words")
+        scales = sb.tile([P, T], U8, name="scales")
+        sharp_rows = sb.tile([P, P], F32, name="sharp_rows")
+        ident = sb.tile([P, P], F32, name="ident")
+
+        nc.vector.memset(scales[:].bitcast(I32), 0)
+        nc.vector.memset(sharp_rows[:], 0.0)
+        nc.vector.memset(mean_sb[:, PACK * U :], 0.0)
+        make_identity(nc, ident[:])
+
+        pts_planes = pts.rearrange("(p t) n -> p t n", t=PACK)
+        nc.sync.dma_start(idx2[:], offs2)
+        nc.sync.dma_start(mean_sb[:, : PACK * U], mean.rearrange("(p t) u -> p (t u)", t=PACK))
+        nc.sync.dma_start(idx[:], offs)
+        nc.sync.dma_start(white_sb[:], white.rearrange("(p t) k -> p t k", t=PACK))
+        nc.sync.dma_start(sharp_rows[0:TILES, :], sharp.rearrange("(j p) o -> j (p o)", p=P))
+        for g in range(4):
+            nc.sync.dma_start(
+                scales[32 * g : 32 * g + 4, :].bitcast(I32), pkpt_scales[0, 4 * g : 4 * g + 4, :].bitcast(I32)
+            )
+        for t in range(PACK):
+            nc.sync.dma_start(planes[t][:], pts_planes[:, t, :])
+        nc.sync.dma_start(query_sb[:], query.rearrange("(p t) q -> p t q", t=PACK))
+        nc.sync.dma_start(words[:].bitcast(I32), pkpt_words[0].rearrange("p n r -> p (n r)").bitcast(I32))
+
+        sharp_ps = psum.tile([P, P], F32, name="sharp_ps", tag="a")
+        nc.tensor.transpose(sharp_ps[:], sharp_rows[:], ident[:])
+        neg_sharp = sb.tile([P, TILES], F32, name="neg_sharp")
+        nc.scalar.activation(neg_sharp[:], sharp_ps[:, 0:TILES], ACT.Copy, scale=-1.0 / K)
+
+        means = []
+        for t in range(PACK):
+            m = sb.tile([P, I], F32, name=f"means{t}")
+            nc.vector.tensor_copy(m[:], mean_sb[:, t * U : t * U + MEAN_WINDOW].indirect(idx2[:]))
+            means.append(m)
+
+        white_bf = sb.tile([P, K, PACK], BF16, name="white_bf", align_bytes=64)
+        nc.scalar.copy(
+            white_bf[:].rearrange("p (c i) t -> p c t i", i=4), white_sb[:].rearrange("p t (c i) -> p c t i", i=4)
+        )
+
+        xc_lo = sb.tile([P, 2, I], F32, name="xc_lo")
+        for t in range(2):
+            nc.vector.tensor_tensor(xc_lo[:, t, :], planes[t][:].indirect(idx[:]), means[t][:], ALU.subtract)
+            if t == 0:
+                white_q = sb.tile([P, K], U32, name="white_q", align_bytes=64)
+                white_s = sb.tile([P, K], U8, name="white_s", align_bytes=64)
+                nc.vector.quantize_mx(white_q[:].bitcast(FP8X4), white_s[:], white_bf[:].rearrange("p k t -> p (k t)"))
+        pk_s = sb.tile([P, I], U8, name="pk_s", align_bytes=64)
+        nc.vector.tensor_copy(pk_s[:], scales[:].indirect(idx[:]))
+
+        xc_bf = [sb.tile([P, P, PACK], BF16, name=f"xc_bf{j}", align_bytes=64) for j in range(TILES)]
+        for j in range(TILES):
+            nc.scalar.copy(xc_bf[j][:, :, 0:2], xc_lo[:, :, j * P : (j + 1) * P].rearrange("p t i -> p i t"))
+
+        xc_hi = [sb.tile([P, 2, P], F32, name=f"xc_hi{j}") for j in range(TILES)]
+        for t in range(2, PACK):
+            for j in range(TILES):
+                nc.vector.tensor_tensor(
+                    xc_hi[j][:, t - 2, :],
+                    planes[t][:].indirect(idx[:, j * COLS : (j + 1) * COLS]),
+                    means[t][:, j * P : (j + 1) * P],
+                    ALU.subtract,
+                )
+        sums = []
+        for j in range(TILES):
+            nc.scalar.copy(xc_bf[j][:, :, 2:4], xc_hi[j][:].rearrange("p t i -> p i t"))
+        for j in range(TILES):
+            xc_q = sb.tile([P, P], U32, name=f"xc_q{j}", align_bytes=64)
+            xc_s = sb.tile([P, P], U8, name=f"xc_s{j}", align_bytes=64)
+            nc.vector.quantize_mx(xc_q[:].bitcast(FP8X4), xc_s[:], xc_bf[j][:].rearrange("p i t -> p (i t)"))
+            z = psum.tile([P, K], F32, name="z")
+            nc.tensor.matmul_mx(
+                z[:], lhsT=xc_q[:].bitcast(FP8X4), lhsT_scale=xc_s[:],
+                rhs=white_q[:].bitcast(FP8X4), rhs_scale=white_s[:], start=True, stop=True,
+            )
+            squares = sb.tile([P, K], F32, name=f"squares{j % 2}")
+            ss = sb.tile([P, 1], F32, name=f"ss{j}")
+            nc.scalar.activation(squares[:], z[:], ACT.Square, accum_out=ss[:])
+            neg_en = sb.tile([P, 1], F32, name=f"neg_en{j}")
+            nc.scalar.activation(neg_en[:], ss[:], ACT.Copy, scale=neg_sharp[:, j : j + 1])
+            sums.append(neg_en)
+
+        query_bf = sb.tile([P, Q, PACK], BF16, name="query_bf", align_bytes=64)
+        nc.vector.tensor_copy(
+            query_bf[:].rearrange("p (c i) t -> p c t i", i=4), query_sb[:].rearrange("p t (c i) -> p c t i", i=4)
+        )
+        query_q = sb.tile([P, Q], U32, name="query_q", align_bytes=64)
+        query_s = sb.tile([P, Q], U8, name="query_s", align_bytes=64)
+        nc.vector.quantize_mx(query_q[:].bitcast(FP8X4), query_s[:], query_bf[:].rearrange("p q t -> p (q t)"))
+
+        for h in range(2):
+            pk_q = sb.tile([P, 2 * P], U32, name=f"pk_q{h}", align_bytes=64)
+            nc.vector.tensor_copy(pk_q[:], words[:].indirect(idx[:, 2 * h * COLS : 2 * (h + 1) * COLS]))
+            for j in range(2 * h, 2 * h + 2):
+                a = psum.tile([P, Q], F32, name="a", tag="a")
+                nc.tensor.matmul_mx(
+                    a[:], lhsT=pk_q[:, (j % 2) * P : (j % 2 + 1) * P].bitcast(FP8X4),
+                    lhsT_scale=pk_s[:, j * P : (j + 1) * P],
+                    rhs=query_q[:].bitcast(FP8X4), rhs_scale=query_s[:], start=True, stop=True,
+                )
+                y = sb.tile([P, Q], F32, name=f"y{j}")
+                if j == 2:
+                    nc.vector.tensor_scalar_add(y[:], a[:], sums[j][:])
+                else:
+                    nc.scalar.activation(y[:], a[:], ACT.Identity, bias=sums[j][:])
+                nc.sync.dma_start(out[j * P : (j + 1) * P, :], y[:])

@@ -31,7 +31,7 @@ def tile_attend_energyscores_kernel(tc, pts, mean, white, pkpt_words, pkpt_scale
 
         idx = sb.tile([P, I // 16], U16, name="idx")
         idx2 = sb.tile([P, I // 16], U16, name="idx2")
-        mean_sb = sb.tile([P, (PACK - 1) * U + MEAN_WINDOW], F32, name="mean_sb")
+        mean_sb = [sb.tile([P, U + MEAN_WINDOW], F32, name=f"mean_sb{h}") for h in range(2)]
         white_sb = sb.tile([P, PACK, K], F32, name="white_sb")
         query_sb = sb.tile([P, PACK, Q], F32, name="query_sb")
         planes = [sb.tile([P, T], F32, name=f"pts{t}") for t in range(PACK)]
@@ -42,17 +42,20 @@ def tile_attend_energyscores_kernel(tc, pts, mean, white, pkpt_words, pkpt_scale
 
         nc.vector.memset(scales[:].bitcast(I32), 0)
         nc.vector.memset(sharp_rows[:], 0.0)
-        nc.vector.memset(mean_sb[:, PACK * U :], 0.0)
+        for h in range(2):
+            nc.vector.memset(mean_sb[h][:, 2 * U :], 0.0)
         make_identity(nc, ident[:])
 
         pts_planes = pts.rearrange("(p t) n -> p t n", t=PACK)
+        mean_rows = mean.rearrange("(p t) u -> p (t u)", t=PACK)
+        nc.sync.dma_start(mean_sb[0][:, : 2 * U], mean_rows[:, : 2 * U])
         nc.sync.dma_start(idx2[:], offs2)
-        nc.sync.dma_start(mean_sb[:, : PACK * U], mean.rearrange("(p t) u -> p (t u)", t=PACK))
+        nc.sync.dma_start(mean_sb[1][:, : 2 * U], mean_rows[:, 2 * U :])
         nc.sync.dma_start(idx[:], offs)
         nc.sync.dma_start(white_sb[:], white.rearrange("(p t) k -> p t k", t=PACK))
-        nc.sync.dma_start(sharp_rows[0:TILES, :], sharp.rearrange("(j p) o -> j (p o)", p=P))
+        nc.gpsimd.dma_start(sharp_rows[0:TILES, :], sharp.rearrange("(j p) o -> j (p o)", p=P))
         for g in range(4):
-            nc.sync.dma_start(
+            nc.gpsimd.dma_start(
                 scales[32 * g : 32 * g + 4, :].bitcast(I32), pkpt_scales[0, 4 * g : 4 * g + 4, :].bitcast(I32)
             )
         for t in range(PACK):
@@ -68,7 +71,7 @@ def tile_attend_energyscores_kernel(tc, pts, mean, white, pkpt_words, pkpt_scale
         means = []
         for t in range(PACK):
             m = sb.tile([P, I], F32, name=f"means{t}")
-            nc.vector.tensor_copy(m[:], mean_sb[:, t * U : t * U + MEAN_WINDOW].indirect(idx2[:]))
+            nc.vector.tensor_copy(m[:], mean_sb[t // 2][:, t % 2 * U : t % 2 * U + MEAN_WINDOW].indirect(idx2[:]))
             means.append(m)
 
         white_bf = sb.tile([P, K, PACK], BF16, name="white_bf", align_bytes=64)
@@ -114,9 +117,7 @@ def tile_attend_energyscores_kernel(tc, pts, mean, white, pkpt_words, pkpt_scale
             squares = sb.tile([P, K], F32, name=f"squares{j % 2}")
             ss = sb.tile([P, 1], F32, name=f"ss{j}")
             nc.scalar.activation(squares[:], z[:], ACT.Square, accum_out=ss[:])
-            neg_en = sb.tile([P, 1], F32, name=f"neg_en{j}")
-            nc.scalar.activation(neg_en[:], ss[:], ACT.Copy, scale=neg_sharp[:, j : j + 1])
-            sums.append(neg_en)
+            sums.append(ss)
 
         query_bf = sb.tile([P, Q, PACK], BF16, name="query_bf", align_bytes=64)
         nc.vector.tensor_copy(
@@ -137,8 +138,12 @@ def tile_attend_energyscores_kernel(tc, pts, mean, white, pkpt_words, pkpt_scale
                     rhs=query_q[:].bitcast(FP8X4), rhs_scale=query_s[:], start=True, stop=True,
                 )
                 y = sb.tile([P, Q], F32, name=f"y{j}")
-                if j == 2:
-                    nc.vector.tensor_scalar_add(y[:], a[:], sums[j][:])
+                if j in (0, 3):
+                    nc.vector.scalar_tensor_tensor(
+                        y[:], neg_sharp[:, j : j + 1].to_broadcast([P, Q]), sums[j][:], a[:], ALU.mult, ALU.add
+                    )
                 else:
-                    nc.scalar.activation(y[:], a[:], ACT.Identity, bias=sums[j][:])
+                    neg_en = sb.tile([P, 1], F32, name=f"neg_en{j}")
+                    nc.gpsimd.tensor_tensor(neg_en[:], sums[j][:], neg_sharp[:, j : j + 1], ALU.mult)
+                    nc.scalar.activation(y[:], a[:], ACT.Identity, bias=neg_en[:])
                 nc.sync.dma_start(out[j * P : (j + 1) * P, :], y[:])

from contextlib import ExitStack

import concourse.mybir as mybir
from concourse.masks import make_identity

D, K, T, I, U, Q = 512, 512, 2048, 512, 256, 256
FLOPS = 2 * I * D * (K + Q)

F32 = mybir.dt.float32
BF16 = mybir.dt.bfloat16
I32 = mybir.dt.int32
U32 = mybir.dt.uint32
U16 = mybir.dt.uint16
U8 = mybir.dt.uint8
FP8X4 = mybir.dt.float8_e4m3fn_x4
ALU = mybir.AluOpType
ACT = mybir.ActivationFunctionType

P = 128
PACK = 4
TILES = I // P
COLS = P // 16
MEAN_WINDOW = 704


def tile_attend_energyscores_kernel(tc, pts, mean, white, pkpt_words, pkpt_scales, query, sharp, offs, offs2, out):
    nc = tc.nc
    with ExitStack() as ctx:
        sb = ctx.enter_context(tc.tile_pool(name="sb", bufs=1))
        psum = ctx.enter_context(tc.psum_pool(name="psum", bufs=4))

        idx = sb.tile([P, I // 16], U16, name="idx")
        idx2 = sb.tile([P, I // 16], U16, name="idx2")
        mean_sb = [sb.tile([P, U + MEAN_WINDOW], F32, name=f"mean_sb{h}") for h in range(2)]
        white_sb = sb.tile([P, PACK, K], F32, name="white_sb")
        query_sb = sb.tile([P, PACK, Q], F32, name="query_sb")
        planes = [sb.tile([P, T], F32, name=f"pts{t}") for t in range(PACK)]
        words = sb.tile([P, T], U32, name="words")
        scales = sb.tile([P, T], U8, name="scales")
        sharp_rows = sb.tile([P, P], F32, name="sharp_rows")
        ident = sb.tile([P, P], F32, name="ident")

        nc.vector.memset(scales[:].bitcast(I32), 0)
        nc.vector.memset(sharp_rows[:], 0.0)
        for h in range(2):
            nc.vector.memset(mean_sb[h][:, 2 * U :], 0.0)
        make_identity(nc, ident[:])

        pts_planes = pts.rearrange("(p t) n -> p t n", t=PACK)
        mean_rows = mean.rearrange("(p t) u -> p (t u)", t=PACK)
        nc.sync.dma_start(mean_sb[0][:, : 2 * U], mean_rows[:, : 2 * U])
        nc.sync.dma_start(idx2[:], offs2)
        nc.sync.dma_start(mean_sb[1][:, : 2 * U], mean_rows[:, 2 * U :])
        nc.sync.dma_start(idx[:], offs)
        nc.sync.dma_start(white_sb[:], white.rearrange("(p t) k -> p t k", t=PACK))
        nc.gpsimd.dma_start(sharp_rows[0:TILES, :], sharp.rearrange("(j p) o -> j (p o)", p=P))
        for g in range(4):
            nc.gpsimd.dma_start(
                scales[32 * g : 32 * g + 4, :].bitcast(I32), pkpt_scales[0, 4 * g : 4 * g + 4, :].bitcast(I32)
            )
        for t in range(PACK):
            nc.sync.dma_start(planes[t][:], pts_planes[:, t, :])
        nc.sync.dma_start(query_sb[:], query.rearrange("(p t) q -> p t q", t=PACK))
        nc.sync.dma_start(words[:].bitcast(I32), pkpt_words[0].rearrange("p n r -> p (n r)").bitcast(I32))

        sharp_ps = psum.tile([P, P], F32, name="sharp_ps", tag="a")
        nc.tensor.transpose(sharp_ps[:], sharp_rows[:], ident[:])
        neg_sharp = sb.tile([P, TILES], F32, name="neg_sharp")
        nc.scalar.activation(neg_sharp[:], sharp_ps[:, 0:TILES], ACT.Copy, scale=-1.0 / K)

        means = []
        for t in range(PACK):
            m = sb.tile([P, I], F32, name=f"means{t}")
            nc.vector.tensor_copy(m[:], mean_sb[t // 2][:, t % 2 * U : t % 2 * U + MEAN_WINDOW].indirect(idx2[:]))
            means.append(m)

        white_bf = sb.tile([P, K, PACK], BF16, name="white_bf", align_bytes=64)
        nc.scalar.copy(
            white_bf[:].rearrange("p (c i) t -> p c t i", i=4), white_sb[:].rearrange("p t (c i) -> p c t i", i=4)
        )

        xc_lo = sb.tile([P, 2, I], F32, name="xc_lo")
        for t in range(2):
            nc.vector.tensor_tensor(xc_lo[:, t, :], planes[t][:].indirect(idx[:]), means[t][:], ALU.subtract)
            if t == 0:
                white_q = sb.tile([P, K], U32, name="white_q", align_bytes=64)
                white_s = sb.tile([P, K], U8, name="white_s", align_bytes=64)
                nc.vector.quantize_mx(white_q[:].bitcast(FP8X4), white_s[:], white_bf[:].rearrange("p k t -> p (k t)"))
        pk_s = sb.tile([P, I], U8, name="pk_s", align_bytes=64)
        nc.vector.tensor_copy(pk_s[:], scales[:].indirect(idx[:]))

        xc_bf = [sb.tile([P, P, PACK], BF16, name=f"xc_bf{j}", align_bytes=64) for j in range(TILES)]
        for j in range(TILES):
            nc.scalar.copy(xc_bf[j][:, :, 0:2], xc_lo[:, :, j * P : (j + 1) * P].rearrange("p t i -> p i t"))

        xc_hi = [sb.tile([P, 2, P], F32, name=f"xc_hi{j}") for j in range(TILES)]
        for t in range(2, PACK):
            for j in range(TILES):
                nc.vector.tensor_tensor(
                    xc_hi[j][:, t - 2, :],
                    planes[t][:].indirect(idx[:, j * COLS : (j + 1) * COLS]),
                    means[t][:, j * P : (j + 1) * P],
                    ALU.subtract,
                )
        sums = []
        for j in range(TILES):
            nc.scalar.copy(xc_bf[j][:, :, 2:4], xc_hi[j][:].rearrange("p t i -> p i t"))
        for j in range(TILES):
            xc_q = sb.tile([P, P], U32, name=f"xc_q{j}", align_bytes=64)
            xc_s = sb.tile([P, P], U8, name=f"xc_s{j}", align_bytes=64)
            nc.vector.quantize_mx(xc_q[:].bitcast(FP8X4), xc_s[:], xc_bf[j][:].rearrange("p i t -> p (i t)"))
            z = psum.tile([P, K], F32, name="z")
            nc.tensor.matmul_mx(
                z[:], lhsT=xc_q[:].bitcast(FP8X4), lhsT_scale=xc_s[:],
                rhs=white_q[:].bitcast(FP8X4), rhs_scale=white_s[:], start=True, stop=True,
            )
            squares = sb.tile([P, K], F32, name=f"squares{j % 2}")
            ss = sb.tile([P, 1], F32, name=f"ss{j}")
            nc.scalar.activation(squares[:], z[:], ACT.Square, accum_out=ss[:])
            sums.append(ss)

        query_bf = sb.tile([P, Q, PACK], BF16, name="query_bf", align_bytes=64)
        nc.vector.tensor_copy(
            query_bf[:].rearrange("p (c i) t -> p c t i", i=4), query_sb[:].rearrange("p t (c i) -> p c t i", i=4)
        )
        query_q = sb.tile([P, Q], U32, name="query_q", align_bytes=64)
        query_s = sb.tile([P, Q], U8, name="query_s", align_bytes=64)
        nc.vector.quantize_mx(query_q[:].bitcast(FP8X4), query_s[:], query_bf[:].rearrange("p q t -> p (q t)"))

        for h in range(2):
            pk_q = sb.tile([P, 2 * P], U32, name=f"pk_q{h}", align_bytes=64)
            nc.vector.tensor_copy(pk_q[:], words[:].indirect(idx[:, 2 * h * COLS : 2 * (h + 1) * COLS]))
            for j in range(2 * h, 2 * h + 2):
                a = psum.tile([P, Q], F32, name="a", tag="a")
                nc.tensor.matmul_mx(
                    a[:], lhsT=pk_q[:, (j % 2) * P : (j % 2 + 1) * P].bitcast(FP8X4),
                    lhsT_scale=pk_s[:, j * P : (j + 1) * P],
                    rhs=query_q[:].bitcast(FP8X4), rhs_scale=query_s[:], start=True, stop=True,
                )
                y = sb.tile([P, Q], F32, name=f"y{j}")
                if j in (0, 3):
                    nc.vector.scalar_tensor_tensor(
                        y[:], neg_sharp[:, j : j + 1].to_broadcast([P, Q]), sums[j][:], a[:], ALU.mult, ALU.add
                    )
                else:
                    neg_en = sb.tile([P, 1], F32, name=f"neg_en{j}")
                    nc.gpsimd.tensor_tensor(neg_en[:], sums[j][:], neg_sharp[:, j : j + 1], ALU.mult)
                    nc.scalar.activation(y[:], a[:], ACT.Identity, bias=neg_en[:])
                nc.sync.dma_start(out[j * P : (j + 1) * P, :], y[:])
